import numpy as np, ml_dtypes
CORES = [40,64,80,88,96,104,120,144]
N = 8
BF = ml_dtypes.bfloat16
def gentries(a):
    return np.ascontiguousarray(a.reshape(8, 16, -1).transpose(0, 2, 1)).reshape(8, -1)
def gtable(e):
    e = np.asarray(e); return np.ascontiguousarray(e.reshape(8, -1, 16).transpose(0, 2, 1)).reshape(128, -1).astype(np.int32)
V, G, H, Q, ST = 1536, 512, 3, 4, 4
W = V + H * G
def come(v, snd):
    return np.concatenate([np.take_along_axis(np.roll(v, -d, axis=0), np.roll(snd[:, :, d - 1], -d, axis=0), 2) for d in range(1, H + 1)], axis=2)
def some(rng):
    return np.ascontiguousarray(np.argsort(rng.random((N, 8, H, V)), axis=-1)[..., :G])
def traffic(rng):
    snd = some(rng); pace = rng.permutation(np.array([2, 3, 4, 4, 6, 8, 8, 16])).reshape(1, 8, 1)
    base = 64 + (rng.random((N, 8, V)) * W * pace).astype(np.int64)
    lane = (rng.random((N, 8, V)) < 0.3 + 0.4 * rng.random((1, 8, 1))).astype(np.int64)
    pw = np.concatenate([base, come(base, snd)], axis=2); lw = np.concatenate([lane, come(lane, snd)], axis=2)
    la = np.zeros((N, 8, V), np.int64); lb = np.zeros((N, 8, V), np.int64)
    for q in range(N):
        for g in range(8):
            order = np.argsort(pw[q, g], kind="stable"); l = lw[q, g][order]; two = []
            for c in (0, 1):
                m = order[l == c]; i = np.searchsorted(pw[q, g][m], base[q, g], side="right"); two.append(m[np.minimum(i, len(m) - 1)])
            la[q, g] = np.where(lane[q, g] == 0, two[0], two[1]); lb[q, g] = np.where(lane[q, g] == 0, two[1], two[0])
    return jitter(rng, base), la, lb, snd
def jitter(rng, base):
    off = rng.integers(0, 2 ** 19, (1, 8, 16, 1)); size = rng.choice(np.array([1.0, 2.0, 4.0]), (N, 8, 1, 1))
    return np.clip(base[:, :, None, :] + off + np.rint(rng.standard_normal((N, 8, 16, V)) * size).astype(np.int64), 0, 2 ** 20 - 1)
def stray(rng, ptr, share):
    return np.where(rng.random(ptr.shape) < share, rng.integers(0, W, ptr.shape), ptr)
def pack(x, la, lb, snd):
    return {"x0": np.ascontiguousarray(x.reshape(N, 128, V)).astype(np.int32), "la": la.astype(np.int32), "lb": lb.astype(np.int32),
            "snd": np.stack([gtable(s.reshape(8, -1)) for s in snd])}
def setup_inputs(rng):
    x, la, lb, snd = traffic(rng)
    return pack(x, stray(rng, la, 0.1), stray(rng, lb, 0.1), snd)
def setup_inputs_ties(rng):
    snd = some(rng); x = np.zeros((N, 8, 16, V), np.int64); la = np.zeros((N, 8, V), np.int64); lb = np.zeros((N, 8, V), np.int64); h = V // 2
    for q in range(N):
        for g in range(8):
            o = rng.permutation(V); fa, fb, fo = o[0:h:2], o[1:h:2], o[h:]; n = h // 2
            xa = rng.integers(2 ** 10, 2 ** 19, (16, n)); cnt = rng.choice(np.array([0, 8, 9, 10, 16]), n)
            xb = xa + 4 + (np.argsort(rng.random((16, n)), axis=0) < cnt)
            i = rng.integers(0, n, V - h); c = rng.choice(np.array([0, 0, 7, 8, 9, 16]), V - h)
            e = np.where(c == 0, rng.integers(1, 15, (16, V - h)), (np.argsort(rng.random((16, V - h)), axis=0) >= c).astype(np.int64))
            x[q, g][:, fa] = xa; x[q, g][:, fb] = xb; x[q, g][:, fo] = xb[:, i] - e
            la[q, g] = np.arange(V); lb[q, g] = np.arange(V)
            la[q, g, fo] = stray(rng, fa[i], 0.125); lb[q, g, fo] = stray(rng, fb[i], 0.125)
    return pack(x, la, lb, snd)
def setup_inputs_weave(rng):
    snd = some(rng); base = 64 + rng.integers(0, 2 ** 15, (N, 8, V)); pw = np.concatenate([base, come(base, snd)], axis=2)
    la = np.zeros((N, 8, V), np.int64); lb = np.zeros((N, 8, V), np.int64)
    for q in range(N):
        for g in range(8):
            order = np.argsort(pw[q, g], kind="stable"); cand = order if g % 4 < 2 else order[(order < V) & (order % Q == 0)]; n = len(cand)
            la[q, g] = cand[rng.integers(0, n, V)]; hi = cand[rng.integers(2 * n // 3, n, V)]; lo = cand[rng.integers(0, n // 3, V)]
            lb[q, g] = hi if g % 2 == 0 else np.where(rng.random(V) < 0.5, hi, lo)
    return pack(jitter(rng, base), la, lb, snd)
def setup_inputs_alike(rng):
    x, la, lb, snd = traffic(rng)
    snd[:, ::2] = rng.choice(np.array([0, 3, V // 2, V - 1]), (N, 4, H, G))
    ends = np.array([0, V - 1, V, W - 1])
    la[:, 1] = rng.choice(ends, (N, V)); lb[:, 1] = rng.choice(ends, (N, V))
    la[:, 2] = rng.integers(V, W, (N, V)); lb[:, 2] = rng.integers(V, W, (N, V))
    la[:, 3] = rng.integers(0, V, (N, V)); lb[:, 3] = la[:, 3]
    lb[:, 4] = np.arange(V)
    x[:, 5] = rng.integers(0, 2 ** 20, (1, 16, 1))
    la[:, 6] = rng.choice(ends)
    return pack(x, la, lb, snd)
def setup_inputs_crowd(rng):
    snd = some(rng); x = rng.integers(0, 2 ** 20, (N, 8, 16, V)); la = rng.integers(0, W, (N, 8, V)); lb = rng.integers(0, W, (N, 8, V)); v = np.arange(V)
    for q in range(N):
        for g in range(8):
            kind = (q + g) % 4; tu = rng.permutation(v[v % Q == 0]); nt = rng.permutation(v[v % Q != 0]); xx = x[q, g]
            if kind == 0:
                hi, lo = nt[:64], nt[64:128]
                xx[:] = rng.integers(2 ** 17, 2 ** 18, (16, V)); xx[:, lo] = rng.integers(0, 2 ** 16, (16, 64)); xx[:, hi] = rng.integers(2 ** 19, 2 ** 20, (16, 64))
                la[q, g] = rng.choice(lo, V); lb[q, g] = rng.choice(hi, V)
            elif kind == 1:
                one, top = tu[0], nt[:8]
                xx[:] = rng.integers(2 ** 17, 2 ** 18, (16, V)); xx[:, nt[8:10]] = rng.integers(0, 2 ** 16, (16, 2))
                xx[:, one] = rng.integers(2 ** 19, 3 * 2 ** 18, 16); xx[:, top] = rng.integers(3 * 2 ** 18, 2 ** 20, (16, 8))
                la[q, g] = np.where(v % Q == 0, rng.choice(top, V), nt[8]); lb[q, g] = one
                la[q, g, one] = nt[9]; lb[q, g, one] = top[0]
            elif kind == 2:
                o = rng.permutation(V); n = V // 4; fa, fb, fo = o[:n], o[n:2 * n], o[2 * n:]; i = rng.integers(0, n, V - 2 * n)
                far = np.argsort(rng.random((16, 1)), axis=0) < 8
                xa = np.exp2(17 * rng.random((16, n))).astype(np.int64)
                xx[:, fa] = xa; xx[:, fb] = np.where(far, xa + rng.integers(5, 21, (16, n)), rng.integers(3 * 2 ** 18, 2 ** 20, (16, n)))
                xx[:, fo] = np.where(far, 2 ** 20 - np.exp2(18 * rng.random((16, V - 2 * n))).astype(np.int64), rng.integers(2 ** 18, 2 ** 19, (16, V - 2 * n)))
                la[q, g] = v; lb[q, g] = v; la[q, g, fo] = fa[i]; lb[q, g, fo] = fb[i]
    return pack(x, la, lb, snd)
def setup_inputs_spread(rng):
    snd = some(rng)
    x = np.minimum((np.exp2(20 * rng.random((N, 8, 1, V))) * rng.random((N, 8, 16, V))).astype(np.int64), 2 ** 20 - 1)
    end = rng.random((N, 8, 1, V)); x = np.where(end < 0.02, 0, np.where(end > 0.98, 2 ** 20 - 1, x))
    up = rng.choice(np.array([1.0, 1.5, 3.0]), (N, 8, 1)); dn = rng.choice(np.array([1.0, 1.5, 3.0]), (N, 8, 1))
    la = np.minimum((rng.random((N, 8, V)) ** up * W).astype(np.int64), W - 1); lb = W - 1 - np.minimum((rng.random((N, 8, V)) ** dn * W).astype(np.int64), W - 1)
    return pack(x, la, lb, snd)
def check_inputs(d):
    bad = []
    for k, hi in (("x0", 2 ** 20 - 1), ("la", W - 1), ("lb", W - 1), ("snd", V - 1)):
        if np.min(d[k]) < 0 or np.max(d[k]) > hi: bad.append("range of " + k)
    return bad
def reference(x0, la, lb, snd):
    x = x0.astype(np.int64).reshape(N, 8, 16, V); a = la.astype(np.int64); b = lb.astype(np.int64)
    sl = np.stack([gentries(s) for s in snd]).astype(np.int64).reshape(N, 8, H, G)
    turn = np.arange(V) % Q
    own = np.zeros((N, 8, H * G), np.int64) + np.arange(V, W)
    never = np.zeros((N, 8, H * G), bool)
    for t in range(ST):
        w = [x]
        for d in range(1, H + 1):
            q = (np.arange(N) + d) % N
            w.append(np.take_along_axis(x[q], sl[q][:, :, d - 1][:, :, None, :], 3))
        w = np.concatenate(w, axis=3)
        ga = np.take_along_axis(w, a[:, :, None, :], 3) - x; gb = np.take_along_axis(w, b[:, :, None, :], 3) - x
        gone = np.add.reduce((gb <= 0).astype(np.int64), axis=2) >= 9
        ch = (np.add.reduce((gb > ga + 4).astype(np.int64), axis=2) >= 9) & ~gone & (turn == t % Q)
        x = x + np.minimum(np.maximum(ga - 2, 0), 5)
        aw = np.concatenate([a, own], axis=2); cw = np.concatenate([ch, never], axis=2)
        aa = np.take_along_axis(aw, a, 2); ab = np.take_along_axis(aw, b, 2)
        ca = np.take_along_axis(cw, a, 2); cb = np.take_along_axis(cw, b, 2)
        na = np.where(ch | (cb & ~gone), b, np.where(ca, aa, a))
        nb = np.where(ch, a, np.where(gone | cb, ab, b))
        a, b = na, nb
    return {"yx": x.reshape(N, 128, V).astype(np.float32), "ya": a.astype(np.float32), "yb": b.astype(np.float32)}

from concourse.bass import DstId, RemoteDMATransfer
from concourse.mybir import AluOpType as OP, ActivationFunctionType as AF

N, V, GB, H, ST = 8, 1536, 512, 3, 4
K = 4096
SPLIT_B = 768
SPLIT_A = 768
LAST_G, LAST_B, LAST_A = 1024, 0, 992
XCH = 4
EARLY = 1
FIRST = ()

SB, F32, BF, I32, U16 = "sbuf", "float32", "bfloat16", "int32", "uint16"
SCRATCH = {name: (SB, [128] + list(shape), dtype) for names, shape, dtype in (
    ("W0 W1", [3072], F32), ("xs sendf pb", [V], F32), ("xi", [V], I32), ("sndi", [96], I32), ("offS", [96], U16),
    ("send1 send2 send3 land1 land2 land3 G inc M EA EB", [V], BF), ("pa4", [384], F32), ("C", [384], BF), ("enc", [3072], BF),
    ("P Z", [192], I32), ("LH", [2, 192], I32), ("D", [2, 288], BF), ("offX offE", [192], U16), ("offT", [48], U16),
    ("yv", [96], BF), ("bq tq A1", [96], F32), ("AB Tt", [192], F32), ("Tin", [3, 64], I32), ("Tf", [3, 64], F32),
    ("pi", [4], I32), ("col", [8], F32), ("ramp", [144], F32), ("OH OS", [16], F32), ("Z1 ZM ZA ZB ZC", [144], BF),
    ("SEL", [2048], BF), ("If", [128], F32), ("Ib", [512], BF), ("cst", [960], BF)) for name in names.split()}
BANKS = ("X0", "X1", "X2", "G0", "G1", "G2", "B6", "B7")
SCRATCH.update({b: ("psum", [128, 512], F32) for b in BANKS})
SEMAPHORES = (["cV", "cS", "cP", "cG", "sent", "ldS", "ldP", "dEnc", "dTurn", "dOut", "dXs"] + ["ldX%d" % k for k in range(XCH)]
              + ["arr%d_%d" % (e, d) for e in range(ST) for d in range(1, H + 1)])


def routes(cores, topo):
    out, choice, near = {}, [], [0] * N
    far = [0] * N
    for q in range(N):
        src = cores[q]
        cross = []
        for d in range(1, H + 1):
            r = (q - d) % N
            if topo.may_write(src, cores[r]):
                out[(q, d)] = None
                near[r] += 1
            else:
                cross.append(d)
        choice.append(cross)
    best = None
    two = [q for q in range(N) if len(choice[q]) >= 2]
    for bits in range(1 << len(two)):
        nr, fr, pick = list(near), list(far), {}
        for q in range(N):
            cross = list(choice[q])
            if q in two and bits >> two.index(q) & 1:
                cross.reverse()
            for j, d in enumerate(cross):
                r = (q - d) % N
                pick[(q, d)] = j % 2 == 0
                if not topo.mates(cores[q], cores[r]):
                    if j % 2 == 0:
                        fr[r] += 1
                    else:
                        nr[r] += 1
        score = sorted(nr + fr, reverse=True)
        if best is None or score < best[0]:
            best = (score, pick)
    for (q, d), other in best[1].items():
        src, dst = cores[q], cores[(q - d) % N]
        able = [c for c in topo.cores_of(src) if c not in cores and topo.may_write(c, dst) and (topo.die(c) != topo.die(src)) == other]
        out[(q, d)] = able[:2]
    return out


def bits_of(engines):
    m = 0
    for e in engines:
        m |= 1 << e
    return m


def landing(T, e, d, lo, hi):
    if e == 0:
        return T.W0[:, V + (d - 1) * GB + lo:V + (d - 1) * GB + hi]
    return T["land%d" % e][:, (d - 1) * GB + lo:(d - 1) * GB + hi]


def first_hop(topo, src, relays):
    free = topo.engines(src, relays[0])
    n = len(free) // len(relays)
    return [free[j * n:(j + 1) * n] for j in range(len(relays))]


def order_of(rt, topo, cores, q):
    def key(d):
        via = rt[(q, d)]
        return (via is None, via is not None and topo.mates(cores[q], cores[(q - d) % N]), d)
    return sorted(range(1, H + 1), key=key)


def relay_program(g, core, T, topo, rt):
    cores = T.cores
    jobs = [(q, d) for (q, d), via in sorted(rt.items()) if via and core in via]
    total = 0
    for e in range(ST):
        for q, d in jobs:
            via, dst = rt[(q, d)], cores[(q - d) % N]
            j, w = via.index(core), GB // len(via)
            sem = T.sem["arr%d_%d" % (e, d)]
            g.wait_ge(sem, len(first_hop(topo, cores[q], via)[j]))
            rid, pid = topo.addr(dst, core)
            ap = landing(T, e, d, j * w, (j + 1) * w)
            g.remote_dma(ap, ap, sem, T.sem.sent, pid, rid, topo.mask(core, dst))
            total += len(topo.engines(core, dst))
    if total:
        g.wait_ge(T.sem.sent, total)


def rank_program(g, core, T, topo):
    cores = T.cores
    rt = routes(cores, topo)
    rank = T.rank_of(core)
    if rank is None:
        relay_program(g, core, T, topo, rt)
        return

    Q = {"V": g.vector, "S": g.scalar, "P": g.tensor, "g": g, "y": g.sync}
    known = {q: {} for q in Q}
    count = {}
    writer, readers = {}, {}

    def wait(q, ev):
        sem, val, snap, _q = ev
        if known[q].get(sem, 0) >= val:
            return
        Q[q].wait_ge(T.sem[sem], val)
        for s, v in snap.items():
            if known[q].get(s, 0) < v:
                known[q][s] = v

    def before(q, rd, wr, dma=False):
        need = []
        for t in rd:
            if t in writer and not (writer[t][3] == q and (t in BANKS or q == "P")):
                need.append(writer[t])
        for t in wr:
            for ev in ([writer[t]] if t in writer else []) + readers.get(t, []):
                if dma or ev[3] != q:
                    need.append(ev)
        top = {}
        for ev in need:
            if ev[0] not in top or top[ev[0]][1] < ev[1]:
                top[ev[0]] = ev
        for ev in sorted(top.values(), key=lambda x: -len(x[2])):
            wait(q, ev)

    def after(q, sem, rd, wr, owner):
        snap = dict(known[q])
        snap[sem] = count[sem]
        ev = (sem, count[sem], snap, owner)
        for t in rd:
            readers.setdefault(t, []).append(ev)
        for t in wr:
            writer[t] = ev
            readers[t] = []

    def op(q, rd, wr, call):
        wr = list(wr) + [t for t in rd if t in BANKS]
        before(q, rd, wr)
        sem = "cG" if q == "g" else "c" + q
        count[sem] = count.get(sem, 0) + 1
        call().then_inc(T.sem[sem], 1)
        after(q, sem, rd, wr, q)

    def dmas(sem, items):
        for q, o, i, rd, wr in items:
            before(q, rd, wr, dma=True)
            Q[q].dma_start(o, i).then_inc(T.sem[sem], 16)
            count[sem] = count.get(sem, 0) + 16
        for q, o, i, rd, wr in items:
            after(q, sem, rd, wr, None)

    def arrives(e, d):
        q = (rank + d) % N
        via = rt[(q, d)]
        sem = "arr%d_%d" % (e, d)
        count[sem] = sum(len(topo.engines(c, core)) for c in (via or [cores[q]]))
        writer["W0g%d" % d if e == 0 else "land%d_%d" % (e, d)] = (sem, count[sem], {sem: count[sem]}, None)

    def send(e, d, rd):
        dst, via = cores[(rank - d) % N], rt[(rank, d)]
        buf = T.sendf if e == 0 else T["send%d" % e]
        sem, c0 = T.sem["arr%d_%d" % (e, d)], (d - 1) * GB
        before("g", rd, [])
        if via is None:
            rid, pid = topo.addr(dst, core)
            g.remote_dma(landing(T, e, d, 0, GB), buf[:, c0:c0 + GB], sem, T.sem.sent, pid, rid, topo.mask(core, dst))
            n = len(topo.engines(core, dst))
        else:
            w, tr, n = GB // len(via), [], 0
            for j, eng in enumerate(first_hop(topo, core, via)):
                rid, pid = topo.addr(via[j], core)
                tr.append(RemoteDMATransfer(dst_ids=[DstId(rid=rid, pnc=pid)], dma_engine_mask=bits_of(eng), remote_sem=sem,
                                            src=buf[:, c0 + j * w:c0 + (j + 1) * w], dst=landing(T, e, d, j * w, (j + 1) * w)))
                n += len(eng)
            g.remote_dma_fused(tr, local_sem=T.sem.sent)
        count["sent"] = count.get("sent", 0) + n

    vec, act, pe = g.vector, g.scalar, g.tensor

    def ts(out, in0, s1, s2, o0, o1, rd, wr):
        if s2 is None:
            op("V", rd, wr, lambda: vec.tensor_scalar(out, in0, s1, None, o0))
        else:
            op("V", rd, wr, lambda: vec.tensor_scalar(out, in0, s1, s2, o0, o1))

    def tt(out, a, b, o, rd, wr):
        op("V", rd, wr, lambda: vec.tensor_tensor(out, a, b, o))

    def cp(out, a, rd, wr):
        op("V", rd, wr, lambda: vec.tensor_copy(out, a))

    def fill(out, c, wr):
        op("V", [], wr, lambda: vec.memset(out, c))

    def sc(out, a, rd, wr, bias=None):
        if bias is None:
            op("S", rd, wr, lambda: act.activation(out, a, AF.Copy))
        else:
            op("S", rd, wr, lambda: act.activation(out, a, AF.Identity, bias=bias))

    def mms(items, rd, bank, start=False, stop=False):
        def call():
            last = None
            for j, (o, l, r) in enumerate(items):
                last = pe.matmul(o, l, r, start and j == 0, stop and j == len(items) - 1)
            return last
        op("P", rd, [bank], call)

    send_order = order_of(rt, topo, cores, rank)

    def lateness(d):
        q = (rank + d) % N
        return order_of(rt, topo, cores, q).index(d) + (0 if rt[(q, d)] is None else 2.5)
    come_order = sorted(range(1, H + 1), key=lambda d: (lateness(d), d))
    for e in range(ST):
        for d in range(1, H + 1):
            arrives(e, d)

    I1, I16, I192, IH = (T.Ib[:, 128 * j:128 * (j + 1)] for j in range(4))
    ZERO, CU, CA, CX, CC = T.cst[:, 0:192], T.cst[:, 192:384], T.cst[:, 384:480], T.cst[:, 480:576], T.cst[:, 576:960]
    PB = ["Pa", "Pb"]

    def win(z, i):
        return z[:, 15 - i:143 - i]

    xw = V // XCH
    dmas("ldS", [("S", T.sndi[:], T.snd[:], [], ["sndi"])])
    for k in range(XCH):
        dmas("ldX%d" % k, [("y" if k % 2 == 0 else "S", T.xi[:, k * xw:(k + 1) * xw], T.x0[:, k * xw:(k + 1) * xw], [], ["xi%d" % k])])
    dmas("ldP", [("y", T.Tin[:, :, 32 * ab + 16 * g2:32 * ab + 16 * g2 + 16], src[g2::2, :], [], ["Tin"])
                 for ab, src in enumerate((T.lb, T.la)) for g2 in range(2)])
    op("g", [], ["pi"], lambda: g.iota(T.pi[:, 0:1], [[1, 1]], 0, 1))
    op("g", [], ["ramp"], lambda: g.iota(T.ramp[:], [[1, 144]], 0, 0, allow_small_or_imprecise_dtypes=True))

    fill(T.enc[:], 0.0, ["enc"])
    cp(T.col[:, 0:1], T.pi[:, 0:1], ["pi"], ["c0"])
    ts(T.pi[:, 1:2], T.pi[:, 0:1], 15, None, OP.bitwise_and, None, ["pi"], ["pi1"])
    ts(T.If[:], T.ramp[:, 0:128], T.col[:, 0:1], None, OP.is_equal, None, ["ramp", "c0"], ["If"])
    cp(T.col[:, 1:2], T.pi[:, 1:2], ["pi1"], ["c1"])
    fill(ZERO, 0.0, ["zero"])
    ts(T.col[:, 2:3], T.col[:, 0:1], T.col[:, 1:2], 15.0, OP.subtract, OP.add, ["c0", "c1"], ["c2"])
    ts(T.OS[:], T.ramp[:, 0:16], T.col[:, 1:2], 1.0 / (4 * K), OP.is_equal, OP.mult, ["ramp", "c1"], ["OS"])
    ts(T.Z1[:], T.ramp[:], T.col[:, 2:3], None, OP.is_equal, None, ["ramp", "c2"], ["Z1"])
    cp(T.offS[:], T.sndi[:], ["sndi"], ["offS"])

    own0 = ["W0o0", "W0o1", "W0o2"]
    for k in range(XCH):
        cp(T.W0[:, k * xw:(k + 1) * xw], T.xi[:, k * xw:(k + 1) * xw], ["xi%d" % k], ["W0c%d" % k] + (own0 if k == XCH - 1 else []))
    x_all = ["W0c%d" % k for k in range(XCH)]
    for d in send_order:
        c0, o0 = (d - 1) * GB, (d - 1) * 32
        cp(T.sendf[:, c0:c0 + 256], T.W0[:, 0:V].indirect(T.offS[:, o0:o0 + 16]), x_all + ["offS"], ["sf%da" % d])
        sc(T.sendf[:, c0 + 256:c0 + GB], T.W0[:, 0:V].indirect(T.offS[:, o0 + 16:o0 + 32]), x_all + ["offS"], ["sf%db" % d])
        send(0, d, ["sf%da" % d, "sf%db" % d])

    def base(bank, src, rd, stop=False):
        mms([(T[bank][:], T.If[:], src)], ["If"] + rd, bank, True, stop)

    for k in range(3):
        base("X%d" % k, T.W0[:, 512 * k:512 * (k + 1)], x_all, True)
        sc(T.xs[:, 512 * k:512 * (k + 1)], T.W0[:, 512 * k:512 * (k + 1)], x_all, ["xs%d" % k])
    for k in range(3):
        base("G%d" % k, T.W0[:, 512 * k:512 * (k + 1)], x_all)
    for i in range(16):
        op("S", ["Z1", "OS"], ["SEL"], lambda: act.activation(T.SEL[:, 128 * i:128 * (i + 1)], win(T.Z1, 2), AF.Identity, scale=T.OS[:, i:i + 1]))

    cp(T.Tf[:], T.Tin[:], ["Tin"], ["Tf"])
    for b in range(3):
        op("V", ["Tf"], ["Tt%d" % b], lambda: vec.transpose(T.Tt[:, 64 * b:64 * b + 64], T.Tf[:, b, :]))
    for b in range(3):
        cp(T.P[:, b::3], T.Tt[:, 64 * b:64 * b + 64], ["Tt%d" % b], PB)
    cp(T.offX[:], T.P[:], PB, ["offXa", "offXb"])

    ts(T.D[:, 1, 192:288], T.ramp[:, 0:96], 96.0, None, OP.add, None, ["ramp"], ["Dg"])
    ts(T.D[:, 0, 192:288], T.ramp[:, 0:96], 0.0, T.col[:, 1:2], OP.mult, OP.add, ["ramp", "c1"], ["Dg"])
    for j, c in enumerate((1.0, 16.0, 192.0, -0.5)):
        ts(T.Ib[:, 128 * j:128 * (j + 1)], T.If[:], c, None, OP.mult, None, ["If"], ["Ib"])

    def digits():
        ts(T.LH[:, 0, :], T.P[:], 15, None, OP.bitwise_and, None, PB, ["LH0"])
        ts(T.LH[:, 1, :], T.P[:], 4, None, OP.arith_shift_right, None, PB, ["LH1"])
        cp(T.D[:, :, 0:192], T.LH[:], ["LH0", "LH1"], ["D"])
        dmas("dEnc", [("y", T.enc[0:128:16, :], T.D[:, 0, 96:288], ["D", "Dg"], ["enc"]),
                      ("y", T.enc[1:128:16, :], T.D[:, 1, 96:288], ["D", "Dg"], ["enc"]),
                      ("y", T.enc[2:128:16, :], ZERO, ["zero"], ["enc"])])
        mms([(T.B7[:, 0:192], I192, T.D[:, 0, 0:192]), (T.B7[:, 0:192], I1, T.D[:, 1, 0:192])], ["D", "Ib"], "B7", True, True)

    def lookups():
        cp(T.offE[:], T.B7[:, 0:192], ["B7"], ["offE"])

    def turn_lists(t):
        dmas("dTurn", [("y", T.offT[:, 0:24], T.offX[t:128:4, 0:96], ["offXb"], ["offT"]),
                       ("y", T.offT[:, 24:48], T.offX[t:128:4, 96:192], ["offXa"], ["offT"])])

    turn_lists(0)
    digits()
    for ap, c in ((CU, -float(K)), (CA, -3.0 * K), (CX, -480.0 * K), (CC, -64.0 * K)):
        fill(ap, c, ["cst"])
    ts(T.OH[:], T.ramp[:, 0:16], T.col[:, 1:2], None, OP.is_equal, None, ["ramp", "c1"], ["OH"])
    ts(T.ZM[:], T.ramp[:], T.col[:, 2:3], 64.0 * K, OP.is_equal, OP.mult, ["ramp", "c2"], ["ZM"])
    lookups()
    ts(T.col[:, 3:4], T.OH[:, 1:2], 16.0, T.OH[:, 0:1], OP.mult, OP.add, ["OH"], ["c3"])
    ts(T.col[:, 5:6], T.OH[:, 2:3], 500.0 * K, None, OP.mult, None, ["OH"], ["c5"])
    ts(T.col[:, 6:7], T.OH[:, 2:3], 64.0 * K, T.col[:, 3:4], OP.mult, OP.add, ["OH", "c3"], ["c6"])
    ts(T.col[:, 4:5], T.OH[:, 2:3], 4.0 * K, T.col[:, 3:4], OP.mult, OP.add, ["OH", "c3"], ["c4"])
    ts(T.ZC[:], T.ramp[:], T.col[:, 2:3], T.col[:, 5:6], OP.is_equal, OP.mult, ["ramp", "c2", "c5"], ["ZC"])
    ts(T.ZA[:], T.ramp[:], T.col[:, 2:3], T.col[:, 4:5], OP.is_equal, OP.mult, ["ramp", "c2", "c4"], ["ZA"])
    ts(T.ZB[:], T.ramp[:], T.col[:, 2:3], T.col[:, 6:7], OP.is_equal, OP.mult, ["ramp", "c2", "c6"], ["ZB"])

    for t in range(ST):
        last = t == ST - 1
        wn, nn = "W%d" % (t % 2), "W%d" % ((t + 1) % 2)
        w, wx = T[wn], T[nn]
        whole = [wn + "o%d" % k for k in range(3)] + [wn + "g%d" % d for d in range(1, H + 1)] + (x_all if t == 0 else [])
        rows = [4 * q + t for q in range(4)]
        cur = ["XG"[t % 2] + str(k) for k in range(3)]
        oth = ["XG"[(t + 1) % 2] + str(k) for k in range(3)]

        def gaps(lo, hi, tok):
            tt(T.G[:, lo:hi], w[:, 0:3072].indirect(T.offX[:, 96 + lo // 16:96 + hi // 16]), T.xs[:, lo:hi], OP.subtract,
               whole + ["offXa", "xs0", "xs1", "xs2"], [tok])

        def clip():
            ts(T.inc[:], T.G[:], 2.0, 7.0, OP.max, OP.min, ["Ga", "Gb"], ["inc"])

        def pick(d, by_vector):
            c0, o0 = (d - 1) * GB, (d - 1) * 32
            tok, out = "s%d_%d" % (t + 1, d), T["send%d" % (t + 1)][:, c0:c0 + GB]
            if by_vector:
                ts(out, T.G[:, 0:V].indirect(T.offS[:, o0:o0 + 32]), 2.0, 7.0, OP.max, OP.min, ["Ga", "offS"], [tok])
            else:
                sc(out, T.inc[:, 0:V].indirect(T.offS[:, o0:o0 + 32]), ["inc", "offS"], [tok])
            send(t + 1, d, [tok])

        def grow(k):
            mms([(T[oth[k]][:], I1, T.inc[:, 512 * k:512 * (k + 1)])], ["inc", "Ib"], oth[k], False, True)

        def keep(k):
            cols = slice(512 * k, 512 * (k + 1))
            sc(wx[:, cols], T[oth[k]][:], [oth[k]], [nn + "o%d" % k], -2.0 * ST if last else None)
            if last:
                dmas("dOut", [("y", T.yx[:, cols], wx[:, cols], [nn + "o%d" % k], [])])
            else:
                dmas("dXs", [("y", T.xs[:, cols], wx[:, cols], [nn + "o%d" % k], ["xs%d" % k])])

        def ghost_base(j):
            d = come_order[j]
            if not last:
                base(cur[j], w[:, V + (d - 1) * GB:V + d * GB], [wn + "g%d" % d])

        def ghost_grow(j):
            d = come_order[j]
            mms([(T[cur[j]][:], I1, T["land%d" % (t + 1)][:, (d - 1) * GB:d * GB])], ["land%d_%d" % (t + 1, d), "Ib"], cur[j], False, True)

        def ghost_keep(j):
            d = come_order[j]
            sc(wx[:, V + (d - 1) * GB:V + d * GB], T[cur[j]][:], [cur[j]], [nn + "g%d" % d])

        def behind(k):
            tt(T.M[:, 512 * k:512 * (k + 1)], T.pb[:, 512 * k:512 * (k + 1)], T[cur[k]][:], OP.is_gt, ["pb", cur[k]], ["M%d" % k])

        def look(name, o0, split):
            if split > 0:
                cp(T[name][:, 0:split], T.enc[:, 0:3072].indirect(T.offE[:, o0:o0 + split // 16]), ["enc", "offE"], [name + "0"])
            sc(T[name][:, split:V], T.enc[:, 0:3072].indirect(T.offE[:, o0 + split // 16:o0 + 96]), ["enc", "offE"], [name + "1"])

        if t > 0:
            turn_lists(t)
        if last:
            digits()
            gaps(0, LAST_G, "Ga")
        else:
            gaps(0, V, "Ga")
        sc(T.pb[:], w[:, 0:3072].indirect(T.offX[:, 0:96]), whole + ["offXb"], ["pb"])
        if t > 0:
            for k in range(3):
                base(oth[k], w[:, 512 * k:512 * (k + 1)], [wn + "o%d" % k])
        ahead = 1 if t in FIRST else 0
        if not last:
            for d in send_order[:ahead]:
                pick(d, True)
            clip()
        sc(T.pa4[:], w[:, 0:3072].indirect(T.offT[:, 24:48]), whole + ["offT"], ["pa4"], 4.0)
        if not last:
            for d in send_order[ahead:]:
                pick(d, False)
            for k in range(3):
                grow(k)
        behind(0)
        ghost_base(0)
        if 0 < t < ST - 1:
            digits()
        if not last:
            for k in range(3):
                keep(k)
        mms([(T.B6[:, 0:384], T.SEL[:, 0:128], CC)], ["SEL", "cst"], "B6", True, False)
        behind(1)
        if t > 0:
            lookups()
        ghost_base(1)
        behind(2)
        mms([(T.B7[:, 192:288], I1, CX)] + [(T.B7[:, 192:288], win(T.ZM, i), T.M[:, i::16]) for i in range(16)],
            ["M0", "M1", "M2", "ZM", "cst", "Ib"], "B7", True, True)
        tt(T.C[:], w[:, 0:3072].indirect(T.offT[:, 0:24]), T.pa4[:], OP.is_gt, whole + ["offT", "pa4"], ["C"])
        mms([(T.B6[:, 24 * i:24 * i + 24], win(T.Z1, 2), T.C[:, i::16]) for i in range(16)], ["C", "Z1"], "B6")
        ts(T.yv[:], T.B7[:, 192:288], -32.0 * K, 32.0 * K, OP.max, OP.min, ["B7"], ["yv"])
        mms([(T.B6[:, 96 * q:96 * q + 96], T.SEL[:, 128 * i:128 * (i + 1)], T.yv[:]) for q, i in enumerate(rows)],
            ["yv", "SEL"], "B6", False, True)
        ghost_base(2)
        tt(T.bq[:], T.P[:, 0:96], T.yv[:], OP.add, ["Pb", "yv"], ["bq"])
        for q, i in enumerate(rows):
            tt(T.enc[:, 192 * i:192 * i + 96], T.enc[:, 192 * i:192 * i + 96], T.B6[:, 96 * q:96 * q + 96], OP.max,
               ["B6"] + (["enc"] if q == 0 else []), ["enc"])
        if last:
            gaps(LAST_G, V, "Gb")
            clip()
        look("EB", 0, LAST_B if last else SPLIT_B)
        look("EA", 96, LAST_A if last else SPLIT_A)
        mms([(T.B7[:, 0:192], I1, CU),
             (T.B7[:, 0:96], I1, T.D[:, 0, 96:192]), (T.B7[:, 0:96], I16, T.D[:, 1, 96:192]),
             (T.B7[:, 96:192], I1, T.D[:, 0, 0:96]), (T.B7[:, 96:192], I16, T.D[:, 1, 0:96])]
            + [(T.B7[:, 96 * h:96 * h + 96], win(T.ZC, i), T.enc[:, 192 * i:192 * i + 96]) for h in range(2) for i in rows],
            ["D", "enc", "ZC", "cst", "Ib"], "B7", True, True)
        if last:
            for k in range(3):
                grow(k)
        else:
            for j in range(EARLY):
                ghost_grow(j)
        mms([(T.B7[:, 288:384], IH, T.yv[:])] + [(T.B7[:, 288:384], win(T.ZB, i), T.EB[:, i::16]) for i in range(16)],
            ["yv", "EB0", "EB1", "ZB", "Ib"], "B7", True, True)
        if last:
            for k in range(3):
                keep(k)
        else:
            for j in range(EARLY, min(EARLY + 1, H)):
                ghost_grow(j)
        mms([(T.B6[:, 0:96], I1, CA)] + [(T.B6[:, 0:96], win(T.ZA, i), T.EA[:, i::16]) for i in range(16)],
            ["EA0", "EA1", "ZA", "cst", "Ib"], "B6", True, True)
        if not last:
            for j in range(EARLY + 1, H):
                ghost_grow(j)
            for j in range(H):
                ghost_keep(j)
        tt(T.AB[:], T.P[:], T.B7[:, 0:192], OP.max, PB + ["B7"], ["AB"])
        tt(T.tq[:], T.bq[:], T.B7[:, 288:384], OP.min, ["bq", "B7"], ["tq"])
        tt(T.Z[:, 0:96], T.AB[:, 0:96], T.B7[:, 288:384], OP.max, ["AB", "B7"], ["Zb"])
        tt(T.A1[:], T.AB[:, 96:192], T.tq[:], OP.max, ["AB", "tq"], ["A1"])
        ts(T.P[:, 0:96], T.Z[:, 0:96], K - 1, None, OP.bitwise_and, None, ["Zb"], ["Pb"])
        if not last:
            cp(T.offX[:, 0:96], T.P[:, 0:96], ["Pb"], ["offXb"])
        tt(T.Z[:, 96:192], T.A1[:], T.B6[:, 0:96], OP.max, ["A1", "B6"], ["Za"])
        ts(T.P[:, 96:192], T.Z[:, 96:192], K - 1, None, OP.bitwise_and, None, ["Za"], ["Pa"])
        if not last:
            cp(T.offX[:, 96:192], T.P[:, 96:192], ["Pa"], ["offXa"])

    for b in range(3):
        cp(T.Tt[:, 64 * b:64 * b + 64], T.P[:, b::3], PB, ["Tt%d" % b])
    for b in range(3):
        op("V", ["Tt%d" % b], ["Tf"], lambda: vec.transpose(T.Tf[:, b, :], T.Tt[:, 64 * b:64 * b + 64]))
    dmas("dOut", [("y" if g2 == 0 else "S", dst[g2::2, :], T.Tf[:, :, 32 * ab + 16 * g2:32 * ab + 16 * g2 + 16], ["Tf"], [])
                  for ab, dst in enumerate((T.yb, T.ya)) for g2 in range(2)])
    for sem in sorted(count):
        g.wait_ge(T.sem[sem], count[sem])
